import numpy as np
import ml_dtypes


def mxq(x, axis, fmt="e4m3"):
    dtype, down = {"e4m3": (ml_dtypes.float8_e4m3fn, 7), "e5m2": (ml_dtypes.float8_e5m2, 14)}[fmt]
    v = np.moveaxis(np.asarray(x, np.float32).astype(ml_dtypes.bfloat16).astype(np.float64), axis, -1)
    blocks = v.reshape(v.shape[:-1] + (-1, 32))
    amax = np.abs(blocks).max(-1, keepdims=True)
    byte = np.maximum(np.where(amax > 0, np.frexp(amax)[1] - 1 + 127, 0) - down, 1)
    scale = np.exp2(byte - 127.0)
    codes = (blocks / scale).astype(np.float32).astype(dtype).astype(np.float64)
    return np.moveaxis((codes * scale).reshape(v.shape), -1, axis)


WIDE = False


def mx_kscale(k):
    if not WIDE:
        return np.ones(k)
    levels = np.array([10, -10, 5, -5, 0])
    if k % 512:
        return np.exp2(np.random.permutation(np.resize(levels, k // 32))).repeat(32)
    a = np.empty((k // 512, 16))
    for p in range(k // 512):
        a[p, :8] = np.random.permutation(np.resize(levels, 8))
        for g in range(8):
            far = levels[np.abs(levels - a[p, g]) >= 10]
            a[p, g + 8] = far[np.random.randint(len(far))]
    return np.exp2(a.ravel()).repeat(32)


def f64(x):
    return np.asarray(x).astype(np.float64)


def striped(idx):
    return np.tile(idx.reshape(-1, 16).T, (8, 1)).astype(np.uint16)


def unstriped(offs):
    return offs[:16].T.reshape(-1).astype(np.int64)


E2M1 = np.array([0.0, 0.5, 1.0, 1.5, 2.0, 3.0, 4.0, 6.0, -0.0, -0.5, -1.0, -1.5, -2.0, -3.0, -4.0, -6.0])


def pack_weight(w, fmt):
    k, n = w.shape
    w = f64(np.asarray(w, np.float32).astype(ml_dtypes.bfloat16)).reshape(k // 32, 32, n)
    amax = np.abs(w).max(1)
    if fmt == "e4m3":
        byte = np.frexp(amax)[1] - 1 + 127 - 7
    else:
        mant, ex = np.frexp(amax / 6.0)
        byte = np.where(mant > 0.5, ex, ex - 1) + 127
    byte = np.clip(np.where(amax > 0, byte, 1), 1, 254)
    scaled = (w * np.exp2(127.0 - byte)[:, None, :]).reshape(k, n).astype(np.float32)
    by_word = np.ascontiguousarray(scaled.reshape(k // 512, 128, 4, n).transpose(0, 1, 3, 2))
    if fmt == "e4m3":
        words = by_word.astype(ml_dtypes.float8_e4m3fn).view(np.uint8)
    else:
        c = by_word.astype(ml_dtypes.float4_e2m1fn).view(np.uint8) & 0xF
        words = (c[..., 0::2] | (c[..., 1::2] << 4)).reshape(k // 512, 128, 2 * n)
    return np.ascontiguousarray(words), np.ascontiguousarray(byte.astype(np.uint8).reshape(k // 512, 16, n))


def unpack_weight(words, scales, fmt):
    g, _, n = scales.shape
    words = np.ascontiguousarray(words).reshape(g, 128, n, -1)
    if fmt == "e4m3":
        vals = words.view(ml_dtypes.float8_e4m3fn).astype(np.float64)
    else:
        nib = np.empty((g, 128, n, 4), np.uint8)
        nib[..., 0::2] = words & 0xF
        nib[..., 1::2] = words >> 4
        vals = E2M1[nib]
    vals = vals * np.repeat(np.exp2(scales.astype(np.float64) - 127.0), 8, axis=1)[..., None]
    return vals.transpose(0, 1, 3, 2).reshape(g * 512, n)


def gelu(v):
    return 0.5 * v * (1.0 + np.tanh(np.sqrt(2.0 / np.pi) * (v + 0.044715 * v**3)))


def striped8(idx):
    return np.concatenate([v.reshape(-1, 16).T for v in idx]).astype(np.uint16)


def unstriped8(offs):
    return np.stack([offs[16 * g:16 * g + 16].T.reshape(-1) for g in range(8)]).astype(np.int64)


def heads(xT, wgt, idx8):
    k = np.arange(xT.shape[0])
    return wgt[k // 4 % 128] * xT[k[:, None], idx8[k % 512 // 64]]


K, T, S, G, R = 512, 2048, 1024, 8, 16

def setup_inputs():
    n = np.random.standard_normal
    s = mx_kscale(K)[:, None]
    xT = 0.5 * n((K, T)) * s
    wgt = np.repeat(np.random.uniform(0.5, 2.0, (G, S)), R, axis=0)
    offs = striped8(np.stack([np.random.permutation(T)[:S] for _ in range(G)]))
    w1 = 0.4 * n((K, K)) / np.sqrt(K) / s / s.T
    w4_words, w4_scales = pack_weight(1.5 * n((K, K)) / np.sqrt(K) / s, "e2m1")
    return {
        "xT": xT.astype(np.float32),
        "wgt": wgt.astype(np.float32),
        "offs": offs,
        "w1": w1.astype(np.float32),
        "w4_words": w4_words,
        "w4_scales": w4_scales,
        "bg": (0.5 * n(K)).astype(np.float32),
        "pri": (0.7 * n(S) - 1.0).astype(np.float32),
    }

def reference(xT, wgt, offs, w1, w4_words, w4_scales, bg, pri):
    xg = mxq(heads(f64(xT), f64(wgt), unstriped8(offs)), 0, "e4m3")
    a = mxq(f64(w1), 0, "e4m3").T @ xg
    g = unpack_weight(w4_words, w4_scales, "e2m1").T @ xg
    h = a / (1.0 + np.exp(-(g + f64(bg)[:, None])))
    y = mxq(h, 0, "e4m3").T @ xg
    return 1.0 / (1.0 + np.exp(-(y + f64(pri)[:, None])))

@@ -1,0 +1,216 @@
+from contextlib import ExitStack
+
+import concourse.mybir as mybir
+from concourse.masks import make_identity
+
+K, T, S = 512, 2048, 1024
+FLOPS = 2 * K * K * S * 2 + 2 * K * S * S
+
+F32 = mybir.dt.float32
+BF16 = mybir.dt.bfloat16
+I32 = mybir.dt.int32
+U32 = mybir.dt.uint32
+U16 = mybir.dt.uint16
+U8 = mybir.dt.uint8
+FP8X4 = mybir.dt.float8_e4m3fn_x4
+FP4X4 = mybir.dt.float4_e2m1fn_x4
+MULT = mybir.AluOpType.mult
+SIGMOID = mybir.ActivationFunctionType.Sigmoid
+
+P = 128
+PACK = 4
+C = 256
+NCH = S // C
+HALF = 512
+
+
+def tile_list_gated_entity_matching_kernel(tc, xT, wgt, offs, w1, w4_words, w4_scales, bg, pri, out):
+    nc = tc.nc
+    with ExitStack() as ctx:
+        keep = ctx.enter_context(tc.tile_pool(name="keep", bufs=1))
+        ps_g = ctx.enter_context(tc.psum_pool(name="ps_g", bufs=3))
+        ps_a = ctx.enter_context(tc.psum_pool(name="ps_a", bufs=2))
+        ps_y = ctx.enter_context(tc.psum_pool(name="ps_y", bufs=3))
+
+        offsets = keep.tile([P, S // 16], U16, name="offsets")
+        nc.sync.dma_start(offsets[:], offs)
+
+        s4_raw = keep.tile([P, K], U8, name="s4_raw", align_bytes=64)
+        nc.gpsimd.memset(s4_raw[:].bitcast(I32), 0)
+        bg_sb = keep.tile([P, PACK], F32, name="bg_sb")
+        pri_rows = keep.tile([P, P], F32, name="pri_rows")
+        nc.gpsimd.memset(pri_rows[:], 0.0)
+
+        w4_raw = keep.tile([P, 2 * K], U8, name="w4_raw", align_bytes=64)
+        planes_hbm = xT.rearrange("(p t) n -> t p n", t=PACK)
+        wgt_head = keep.tile([P, C], F32, name="wgt_head")
+        wgt_rest = keep.tile([P, S - C], F32, name="wgt_rest")
+        planes = [keep.tile([P, T], F32, name="plane%d" % t) for t in range(PACK)]
+        w1_hbm = w1.rearrange("(p j) r -> p j r", j=PACK)
+        w1_raw = [keep.tile([P, PACK, K // 2], F32, name="w1_raw%d" % u) for u in range(2)]
+        nc.sync.dma_start(wgt_head[:], wgt[:, 0:C])
+        nc.sync.dma_start(planes[0][:], planes_hbm[0])
+        for q in range(4):
+            nc.sync.dma_start(s4_raw[32 * q : 32 * q + 4, :].bitcast(I32), w4_scales[0, 4 * q : 4 * q + 4, :].bitcast(I32))
+        nc.sync.dma_start(w4_raw[:].bitcast(I32), w4_words[0].bitcast(I32))
+        nc.sync.dma_start(wgt_rest[:], wgt[:, C:S])
+        nc.sync.dma_start(planes[1][:], planes_hbm[1])
+        nc.sync.dma_start(bg_sb[:], bg.rearrange("(p t) -> p t", t=PACK))
+        nc.sync.dma_start(pri_rows[0 : S // P, :], pri.rearrange("(c p) -> c p", p=P))
+        nc.sync.dma_start(planes[2][:], planes_hbm[2])
+        nc.sync.dma_start(w1_raw[0][:], w1_hbm[:, :, 0 : K // 2])
+        nc.sync.dma_start(planes[3][:], planes_hbm[3])
+        nc.sync.dma_start(w1_raw[1][:], w1_hbm[:, :, K // 2 : K])
+
+        warm = keep.tile([P, 1], F32, name="warm")
+        nc.vector.memset(warm[:], 0.0)
+        nc.scalar.activation(warm[:], warm[:], SIGMOID)
+
+        ident = keep.tile([P, P], F32, name="ident")
+        make_identity(nc, ident[:])
+        pri_ps = ps_y.tile([P, HALF], F32, name="y")
+        nc.tensor.transpose(pri_ps[:, 0:P], pri_rows[:], ident[:])
+        pri_sb = keep.tile([P, S // P], F32, name="pri_sb")
+        nc.scalar.copy(pri_sb[:], pri_ps[:, 0 : S // P])
+
+        w4_codes = keep.tile([P, 2 * K], U8, name="w4_codes", align_bytes=64)
+        w4_scale = keep.tile([P, K], U8, name="w4_scale", align_bytes=64)
+
+        def order_w4():
+            nc.vector.tensor_copy(
+                w4_codes[:].bitcast(U16).rearrange("p (t m) -> p t m", t=PACK),
+                w4_raw[:].bitcast(U16).rearrange("p (m t) -> p t m", t=PACK),
+            )
+            nc.vector.tensor_copy(
+                w4_scale[:].rearrange("p (t m) -> p t m", t=PACK),
+                s4_raw[:].rearrange("p (m t) -> p t m", t=PACK),
+            )
+
+        picked = [[keep.tile([P, 2, C], F32, name="picked%d_%d" % (u, c)) for c in range(NCH)] for u in range(2)]
+        xb = [keep.tile([P, C, PACK], BF16, name="xb%d" % c, align_bytes=64) for c in range(NCH)]
+        xg_codes = keep.tile([P, S], U32, name="xg_codes", align_bytes=64)
+        xg_scale = keep.tile([P, S], U8, name="xg_scale", align_bytes=64)
+        h_codes = keep.tile([P, S], U32, name="h_codes", align_bytes=64)
+        h_scale = keep.tile([P, S], U8, name="h_scale", align_bytes=64)
+        gate = [keep.tile([P, PACK, C], F32, name="gate%d" % c) for c in range(NCH)]
+        hb = [keep.tile([P, P, PACK], BF16, name="hb%d" % b, align_bytes=64) for b in range(S // P)]
+        prob = [keep.tile([P, S], F32, name="prob%d" % b) for b in range(S // P)]
+        w1b = keep.tile([P, PACK, P, PACK], BF16, name="w1b", align_bytes=64)
+        w1_codes = keep.tile([P, K], U32, name="w1_codes", align_bytes=64)
+        w1_scale = keep.tile([P, K], U8, name="w1_scale", align_bytes=64)
+
+        def gather(t, first, count):
+            c, lo = divmod(first, C)
+            weights = wgt_head[:, first : first + count] if c == 0 else wgt_rest[:, first - C : first - C + count]
+            nc.vector.tensor_tensor(
+                picked[t // 2][c][:, t % 2, lo : lo + count],
+                planes[t][:].indirect(offsets[:, first // 16 : (first + count) // 16]),
+                weights,
+                MULT,
+            )
+
+        def weave_low(c):
+            nc.scalar.copy(xb[c][:, :, 0:2], picked[0][c][:].rearrange("p t n -> p n t"))
+
+        def weave_high(c, v):
+            part = slice(v * P, (v + 1) * P)
+            nc.vector.tensor_copy(xb[c][:, part, 2:4], picked[1][c][:, :, part].rearrange("p t n -> p n t"))
+
+        def quant_x(c):
+            cols = slice(c * C, (c + 1) * C)
+            nc.vector.quantize_mx(xg_codes[:, cols].bitcast(FP8X4), xg_scale[:, cols], xb[c][:].rearrange("p n t -> p (n t)"))
+
+        def gates(c):
+            cols = slice(c * C, (c + 1) * C)
+            for u in range(2):
+                g = ps_g.tile([P, 2, C], F32, name="g")
+                for e in range(2):
+                    t = 2 * u + e
+                    nc.tensor.matmul_mx(
+                        g[:, e, :],
+                        lhsT=w4_codes[:, 2 * P * t : 2 * P * (t + 1)].bitcast(FP4X4),
+                        lhsT_scale=w4_scale[:, P * t : P * (t + 1)],
+                        rhs=xg_codes[:, cols].bitcast(FP8X4),
+                        rhs_scale=xg_scale[:, cols],
+                        start=True,
+                        stop=True,
+                    )
+                for e in range(2):
+                    t = 2 * u + e
+                    nc.scalar.activation(gate[c][:, t, :], g[:, e, :], SIGMOID, bias=bg_sb[:, t : t + 1])
+
+        def cast_w1(u):
+            nc.scalar.copy(
+                w1b[:, :, u * P // 2 : (u + 1) * P // 2, :].rearrange("p t m j -> p m j t"),
+                w1_raw[u][:].rearrange("p j (m t) -> p m j t", t=PACK),
+            )
+
+        def quant_w1():
+            nc.vector.quantize_mx(w1_codes[:].bitcast(FP8X4), w1_scale[:], w1b[:].rearrange("p t m j -> p (t m j)"))
+
+        def gated(c, v):
+            cols = slice(c * C + v * P, c * C + (v + 1) * P)
+            a = ps_a.tile([P, PACK, P], F32, name="a")
+            for t in range(PACK):
+                nc.tensor.matmul_mx(
+                    a[:, t, :],
+                    lhsT=w1_codes[:, P * t : P * (t + 1)].bitcast(FP8X4),
+                    lhsT_scale=w1_scale[:, P * t : P * (t + 1)],
+                    rhs=xg_codes[:, cols].bitcast(FP8X4),
+                    rhs_scale=xg_scale[:, cols],
+                    start=True,
+                    stop=True,
+                )
+            nc.vector.tensor_tensor(
+                hb[2 * c + v][:].rearrange("p (b i) t -> p b t i", i=4),
+                a[:].rearrange("p t (b i) -> p b t i", i=4),
+                gate[c][:, :, v * P : (v + 1) * P].rearrange("p t (b i) -> p b t i", i=4),
+                MULT,
+            )
+
+        def quant_h(b):
+            cols = slice(b * P, (b + 1) * P)
+            nc.vector.quantize_mx(h_codes[:, cols].bitcast(FP8X4), h_scale[:, cols], hb[b][:].rearrange("p n t -> p (n t)"))
+
+        def match(b, u):
+            rows = slice(b * P, (b + 1) * P)
+            cols = slice(u * HALF, (u + 1) * HALF)
+            y = ps_y.tile([P, HALF], F32, name="y")
+            nc.tensor.matmul_mx(
+                y[:],
+                lhsT=h_codes[:, rows].bitcast(FP8X4),
+                lhsT_scale=h_scale[:, rows],
+                rhs=xg_codes[:, cols].bitcast(FP8X4),
+                rhs_scale=xg_scale[:, cols],
+                start=True,
+                stop=True,
+            )
+            nc.scalar.activation(prob[b][:, cols], y[:], SIGMOID, bias=pri_sb[:, b : b + 1])
+            if b == S // P - 1:
+                nc.sync.dma_start(out[rows, cols], prob[b][:, cols])
+            elif u == 1:
+                nc.sync.dma_start(out[rows, :], prob[b][:])
+
+        for t in range(3):
+            for c in range(NCH):
+                gather(t, c * C, C)
+                if t == 1:
+                    weave_low(c)
+                if t == 0 and c == 0:
+                    order_w4()
+        cast_w1(0)
+        for c in range(NCH):
+            for v in range(2):
+                gather(3, c * C + v * P, P)
+            for v in range(2):
+                weave_high(c, v)
+            quant_x(c)
+            if c == 0:
+                cast_w1(1)
+            gates(c)
+        quant_w1()
+        for b in range(S // P):
+            gated(b // 2, b % 2)
+            quant_h(b)
+            for u in range(2):
+                match(b, u)

@@ -43,17 +43,16 @@ def tile_list_gated_entity_matching_kernel(tc, xT, wgt, offs, w1, w4_words, w4_s
 
         w4_raw = keep.tile([P, 2 * K], U8, name="w4_raw", align_bytes=64)
         planes_hbm = xT.rearrange("(p t) n -> t p n", t=PACK)
-        wgt_head = keep.tile([P, C], F32, name="wgt_head")
-        wgt_rest = keep.tile([P, S - C], F32, name="wgt_rest")
+        wgt_sb = keep.tile([P, S], F32, name="wgt_sb")
         planes = [keep.tile([P, T], F32, name="plane%d" % t) for t in range(PACK)]
         w1_hbm = w1.rearrange("(p j) r -> p j r", j=PACK)
         w1_raw = [keep.tile([P, PACK, K // 2], F32, name="w1_raw%d" % u) for u in range(2)]
-        nc.sync.dma_start(wgt_head[:], wgt[:, 0:C])
+        nc.sync.dma_start(wgt_sb[:, 0:C], wgt[:, 0:C])
         nc.sync.dma_start(planes[0][:], planes_hbm[0])
+        nc.scalar.dma_start(w4_raw[:].bitcast(I32), w4_words[0].bitcast(I32))
         for q in range(4):
-            nc.sync.dma_start(s4_raw[32 * q : 32 * q + 4, :].bitcast(I32), w4_scales[0, 4 * q : 4 * q + 4, :].bitcast(I32))
-        nc.sync.dma_start(w4_raw[:].bitcast(I32), w4_words[0].bitcast(I32))
-        nc.sync.dma_start(wgt_rest[:], wgt[:, C:S])
+            nc.scalar.dma_start(s4_raw[32 * q : 32 * q + 4, :].bitcast(I32), w4_scales[0, 4 * q : 4 * q + 4, :].bitcast(I32))
+        nc.sync.dma_start(wgt_sb[:, C:S], wgt[:, C:S])
         nc.sync.dma_start(planes[1][:], planes_hbm[1])
         nc.sync.dma_start(bg_sb[:], bg.rearrange("(p t) -> p t", t=PACK))
         nc.sync.dma_start(pri_rows[0 : S // P, :], pri.rearrange("(c p) -> c p", p=P))
@@ -86,7 +85,8 @@ def tile_list_gated_entity_matching_kernel(tc, xT, wgt, offs, w1, w4_words, w4_s
                 s4_raw[:].rearrange("p (m t) -> p t m", t=PACK),
             )
 
-        picked = [[keep.tile([P, 2, C], F32, name="picked%d_%d" % (u, c)) for c in range(NCH)] for u in range(2)]
+        low = [keep.tile([P, 2, HALF], F32, name="low%d" % u) for u in range(2)]
+        high = [keep.tile([P, 2, C], F32, name="high%d" % c) for c in range(NCH)]
         xb = [keep.tile([P, C, PACK], BF16, name="xb%d" % c, align_bytes=64) for c in range(NCH)]
         xg_codes = keep.tile([P, S], U32, name="xg_codes", align_bytes=64)
         xg_scale = keep.tile([P, S], U8, name="xg_scale", align_bytes=64)
@@ -100,21 +100,23 @@ def tile_list_gated_entity_matching_kernel(tc, xT, wgt, offs, w1, w4_words, w4_s
         w1_scale = keep.tile([P, K], U8, name="w1_scale", align_bytes=64)
 
         def gather(t, first, count):
-            c, lo = divmod(first, C)
-            weights = wgt_head[:, first : first + count] if c == 0 else wgt_rest[:, first - C : first - C + count]
-            nc.vector.tensor_tensor(
-                picked[t // 2][c][:, t % 2, lo : lo + count],
-                planes[t][:].indirect(offsets[:, first // 16 : (first + count) // 16]),
-                weights,
-                MULT,
-            )
+            weights = wgt_sb[:, first : first + count]
+            if t < 2:
+                dst = low[first // HALF][:, t, first % HALF : first % HALF + count]
+            else:
+                dst = high[first // C][:, t - 2, first % C : first % C + count]
+            nc.vector.tensor_tensor(dst, planes[t][:].indirect(offsets[:, first // 16 : (first + count) // 16]), weights, MULT)
 
         def weave_low(c):
-            nc.scalar.copy(xb[c][:, :, 0:2], picked[0][c][:].rearrange("p t n -> p n t"))
+            part = slice(c * C % HALF, c * C % HALF + C)
+            nc.scalar.copy(xb[c][:, :, 0:2], low[c * C // HALF][:, :, part].rearrange("p t n -> p n t"))
+
+        def weave_high_scalar(c):
+            nc.scalar.copy(xb[c][:, :, 2:4], high[c][:].rearrange("p t n -> p n t"))
 
         def weave_high(c, v):
             part = slice(v * P, (v + 1) * P)
-            nc.vector.tensor_copy(xb[c][:, part, 2:4], picked[1][c][:, :, part].rearrange("p t n -> p n t"))
+            nc.vector.tensor_copy(xb[c][:, part, 2:4], high[c][:, :, part].rearrange("p t n -> p n t"))
 
         def quant_x(c):
             cols = slice(c * C, (c + 1) * C)
@@ -185,28 +187,40 @@ def tile_list_gated_entity_matching_kernel(tc, xT, wgt, offs, w1, w4_words, w4_s
                 start=True,
                 stop=True,
             )
+            if b == S // P - 1 and u == 1:
+                for q in range(2):
+                    part = slice(HALF + q * C, HALF + (q + 1) * C)
+                    nc.scalar.activation(prob[b][:, part], y[:, q * C : (q + 1) * C], SIGMOID, bias=pri_sb[:, b : b + 1])
+                    nc.sync.dma_start(out[rows, part], prob[b][:, part])
+                return
             nc.scalar.activation(prob[b][:, cols], y[:], SIGMOID, bias=pri_sb[:, b : b + 1])
-            if b == S // P - 1:
+            if b in (0, S // P - 1):
                 nc.sync.dma_start(out[rows, cols], prob[b][:, cols])
             elif u == 1:
                 nc.sync.dma_start(out[rows, :], prob[b][:])
 
-        for t in range(3):
-            for c in range(NCH):
-                gather(t, c * C, C)
-                if t == 1:
-                    weave_low(c)
-                if t == 0 and c == 0:
-                    order_w4()
+        order_w4()
+        gather(0, 0, C)
+        gather(0, C, C)
+        gather(0, HALF, HALF)
+        for u in range(2):
+            gather(1, u * HALF, HALF)
+            weave_low(2 * u)
+            weave_low(2 * u + 1)
+        for c in range(NCH):
+            gather(2, c * C, C)
         cast_w1(0)
         for c in range(NCH):
-            for v in range(2):
-                gather(3, c * C + v * P, P)
-            for v in range(2):
-                weave_high(c, v)
-            quant_x(c)
             if c == 0:
+                gather(3, c * C, C)
+                weave_high_scalar(c)
                 cast_w1(1)
+            else:
+                for v in range(2):
+                    gather(3, c * C + v * P, P)
+                for v in range(2):
+                    weave_high(c, v)
+            quant_x(c)
             gates(c)
         quant_w1()
         for b in range(S // P):

@@ -49,16 +49,16 @@ def tile_list_gated_entity_matching_kernel(tc, xT, wgt, offs, w1, w4_words, w4_s
         w1_raw = [keep.tile([P, PACK, K // 2], F32, name="w1_raw%d" % u) for u in range(2)]
         nc.sync.dma_start(wgt_sb[:, 0:C], wgt[:, 0:C])
         nc.sync.dma_start(planes[0][:], planes_hbm[0])
-        nc.scalar.dma_start(w4_raw[:].bitcast(I32), w4_words[0].bitcast(I32))
         for q in range(4):
-            nc.scalar.dma_start(s4_raw[32 * q : 32 * q + 4, :].bitcast(I32), w4_scales[0, 4 * q : 4 * q + 4, :].bitcast(I32))
+            nc.sync.dma_start(s4_raw[32 * q : 32 * q + 4, :].bitcast(I32), w4_scales[0, 4 * q : 4 * q + 4, :].bitcast(I32))
+        nc.sync.dma_start(w4_raw[:].bitcast(I32), w4_words[0].bitcast(I32))
         nc.sync.dma_start(wgt_sb[:, C:S], wgt[:, C:S])
         nc.sync.dma_start(planes[1][:], planes_hbm[1])
         nc.sync.dma_start(bg_sb[:], bg.rearrange("(p t) -> p t", t=PACK))
         nc.sync.dma_start(pri_rows[0 : S // P, :], pri.rearrange("(c p) -> c p", p=P))
         nc.sync.dma_start(planes[2][:], planes_hbm[2])
-        nc.sync.dma_start(w1_raw[0][:], w1_hbm[:, :, 0 : K // 2])
         nc.sync.dma_start(planes[3][:], planes_hbm[3])
+        nc.sync.dma_start(w1_raw[0][:], w1_hbm[:, :, 0 : K // 2])
         nc.sync.dma_start(w1_raw[1][:], w1_hbm[:, :, K // 2 : K])
 
         warm = keep.tile([P, 1], F32, name="warm")
@@ -111,9 +111,6 @@ def tile_list_gated_entity_matching_kernel(tc, xT, wgt, offs, w1, w4_words, w4_s
             part = slice(c * C % HALF, c * C % HALF + C)
             nc.scalar.copy(xb[c][:, :, 0:2], low[c * C // HALF][:, :, part].rearrange("p t n -> p n t"))
 
-        def weave_high_scalar(c):
-            nc.scalar.copy(xb[c][:, :, 2:4], high[c][:].rearrange("p t n -> p n t"))
-
         def weave_high(c, v):
             part = slice(v * P, (v + 1) * P)
             nc.vector.tensor_copy(xb[c][:, part, 2:4], high[c][:, :, part].rearrange("p t n -> p n t"))
@@ -142,7 +139,7 @@ def tile_list_gated_entity_matching_kernel(tc, xT, wgt, offs, w1, w4_words, w4_s
                     nc.scalar.activation(gate[c][:, t, :], g[:, e, :], SIGMOID, bias=bg_sb[:, t : t + 1])
 
         def cast_w1(u):
-            nc.scalar.copy(
+            (nc.scalar.copy, nc.vector.tensor_copy)[u](
                 w1b[:, :, u * P // 2 : (u + 1) * P // 2, :].rearrange("p t m j -> p m j t"),
                 w1_raw[u][:].rearrange("p j (m t) -> p m j t", t=PACK),
             )
@@ -187,20 +184,14 @@ def tile_list_gated_entity_matching_kernel(tc, xT, wgt, offs, w1, w4_words, w4_s
                 start=True,
                 stop=True,
             )
-            if b == S // P - 1 and u == 1:
-                for q in range(2):
-                    part = slice(HALF + q * C, HALF + (q + 1) * C)
-                    nc.scalar.activation(prob[b][:, part], y[:, q * C : (q + 1) * C], SIGMOID, bias=pri_sb[:, b : b + 1])
-                    nc.sync.dma_start(out[rows, part], prob[b][:, part])
-                return
             nc.scalar.activation(prob[b][:, cols], y[:], SIGMOID, bias=pri_sb[:, b : b + 1])
-            if b in (0, S // P - 1):
+            if b == S // P - 1:
                 nc.sync.dma_start(out[rows, cols], prob[b][:, cols])
             elif u == 1:
                 nc.sync.dma_start(out[rows, :], prob[b][:])
 
-        order_w4()
         gather(0, 0, C)
+        order_w4()
         gather(0, C, C)
         gather(0, HALF, HALF)
         for u in range(2):
@@ -211,18 +202,16 @@ def tile_list_gated_entity_matching_kernel(tc, xT, wgt, offs, w1, w4_words, w4_s
             gather(2, c * C, C)
         cast_w1(0)
         for c in range(NCH):
-            if c == 0:
-                gather(3, c * C, C)
-                weave_high_scalar(c)
-                cast_w1(1)
-            else:
-                for v in range(2):
-                    gather(3, c * C + v * P, P)
-                for v in range(2):
-                    weave_high(c, v)
+            for v in range(2):
+                gather(3, c * C + v * P, P)
+            for v in range(2):
+                weave_high(c, v)
             quant_x(c)
             gates(c)
-        quant_w1()
+            if c == 1:
+                cast_w1(1)
+            if c == 2:
+                quant_w1()
         for b in range(S // P):
             gated(b // 2, b % 2)
             quant_h(b)

@@ -61,10 +61,6 @@ def tile_list_gated_entity_matching_kernel(tc, xT, wgt, offs, w1, w4_words, w4_s
         nc.sync.dma_start(w1_raw[0][:], w1_hbm[:, :, 0 : K // 2])
         nc.sync.dma_start(w1_raw[1][:], w1_hbm[:, :, K // 2 : K])
 
-        warm = keep.tile([P, 1], F32, name="warm")
-        nc.vector.memset(warm[:], 0.0)
-        nc.scalar.activation(warm[:], warm[:], SIGMOID)
-
         ident = keep.tile([P, P], F32, name="ident")
         make_identity(nc, ident[:])
         pri_ps = ps_y.tile([P, HALF], F32, name="y")

@@ -22,6 +22,7 @@ PACK = 4
 C = 256
 NCH = S // C
 HALF = 512
+LAST = S - C
 
 
 def tile_list_gated_entity_matching_kernel(tc, xT, wgt, offs, w1, w4_words, w4_scales, bg, pri, out):
@@ -33,7 +34,13 @@ def tile_list_gated_entity_matching_kernel(tc, xT, wgt, offs, w1, w4_words, w4_s
         ps_y = ctx.enter_context(tc.psum_pool(name="ps_y", bufs=3))
 
         offsets = keep.tile([P, S // 16], U16, name="offsets")
-        nc.sync.dma_start(offsets[:], offs)
+
+        wgt_rows = keep.tile([P, C], F32, name="wgt_rows")
+        half_rows = wgt.rearrange("p (s n) -> (p s) n", s=2)[0 : 2 * P : 17, :]
+        for d in range(2):
+            nc.sync.dma_start(wgt_rows[16 * d : 16 * (d + 1), :], half_rows[:, d * C : (d + 1) * C])
+        nc.vector.memset(wgt_rows[32:64, :], 0.0)
+        nc.vector.memset(wgt_rows[64:P, :], 0.0)
 
         s4_raw = keep.tile([P, K], U8, name="s4_raw", align_bytes=64)
         nc.gpsimd.memset(s4_raw[:].bitcast(I32), 0)
@@ -44,18 +51,17 @@ def tile_list_gated_entity_matching_kernel(tc, xT, wgt, offs, w1, w4_words, w4_s
         w4_raw = keep.tile([P, 2 * K], U8, name="w4_raw", align_bytes=64)
         planes_hbm = xT.rearrange("(p t) n -> t p n", t=PACK)
         wgt_sb = keep.tile([P, S], F32, name="wgt_sb")
-        planes = [keep.tile([P, T], F32, name="plane%d" % t) for t in range(PACK)]
+        planes = [keep.tile([P, T], F32, name="plane%d" % t, align_bytes=64) for t in range(PACK)]
         w1_hbm = w1.rearrange("(p j) r -> p j r", j=PACK)
         w1_raw = [keep.tile([P, PACK, K // 2], F32, name="w1_raw%d" % u) for u in range(2)]
-        nc.sync.dma_start(wgt_sb[:, 0:C], wgt[:, 0:C])
         nc.sync.dma_start(planes[0][:], planes_hbm[0])
+        nc.sync.dma_start(offsets[:], offs)
+        nc.sync.dma_start(w4_raw[:].bitcast(I32), w4_words[0].bitcast(I32))
         for q in range(4):
             nc.sync.dma_start(s4_raw[32 * q : 32 * q + 4, :].bitcast(I32), w4_scales[0, 4 * q : 4 * q + 4, :].bitcast(I32))
-        nc.sync.dma_start(w4_raw[:].bitcast(I32), w4_words[0].bitcast(I32))
-        nc.sync.dma_start(wgt_sb[:, C:S], wgt[:, C:S])
         nc.sync.dma_start(planes[1][:], planes_hbm[1])
-        nc.sync.dma_start(bg_sb[:], bg.rearrange("(p t) -> p t", t=PACK))
         nc.sync.dma_start(pri_rows[0 : S // P, :], pri.rearrange("(c p) -> c p", p=P))
+        nc.sync.dma_start(bg_sb[:], bg.rearrange("(p t) -> p t", t=PACK))
         nc.sync.dma_start(planes[2][:], planes_hbm[2])
         nc.sync.dma_start(planes[3][:], planes_hbm[3])
         nc.sync.dma_start(w1_raw[0][:], w1_hbm[:, :, 0 : K // 2])
@@ -63,44 +69,69 @@ def tile_list_gated_entity_matching_kernel(tc, xT, wgt, offs, w1, w4_words, w4_s
 
         ident = keep.tile([P, P], F32, name="ident")
         make_identity(nc, ident[:])
-        pri_ps = ps_y.tile([P, HALF], F32, name="y")
-        nc.tensor.transpose(pri_ps[:, 0:P], pri_rows[:], ident[:])
-        pri_sb = keep.tile([P, S // P], F32, name="pri_sb")
-        nc.scalar.copy(pri_sb[:], pri_ps[:, 0 : S // P])
 
-        w4_codes = keep.tile([P, 2 * K], U8, name="w4_codes", align_bytes=64)
-        w4_scale = keep.tile([P, K], U8, name="w4_scale", align_bytes=64)
+        wgt_t = ps_y.tile([P, 2, P], F32, name="y")
+        for e in range(2):
+            nc.tensor.transpose(wgt_t[:, e, :], wgt_rows[:, e * P : (e + 1) * P], ident[:])
+        spread = keep.tile([P, S // P, 8, 16], F32, name="spread")
+        for first, count in [(0, 1), (1, 1), (2, 2), (4, 2), (6, 2)]:
+            s, d, e = first // 4, first // 2 % 2, first % 2
+            nc.vector.tensor_copy(
+                spread[:, first : first + count, :, :],
+                wgt_t[:, e : e + count, 16 * d + s : 16 * (d + 1) : 2].unsqueeze(3).to_broadcast([P, count, 8, 16]),
+            )
+        pieces = [(0, 1), (1, 2), (5, 3), (3, 2)]
+        for first, count in pieces:
+            back = ps_g.tile([P, count, P], F32, name="g")
+            for v in range(count):
+                nc.tensor.transpose(back[:, v, :], spread[:, first + v, :, :].rearrange("p g r -> p (g r)"), ident[:])
+            nc.scalar.copy(wgt_sb[:, first * P : (first + count) * P], back[:].rearrange("p v n -> p (v n)"))
+
+        pri_sb = keep.tile([P, S // P], F32, name="pri_sb")
+
+        def turn_pri():
+            pri_ps = ps_g.tile([P, HALF], F32, name="g")
+            nc.tensor.transpose(pri_ps[:, 0:P], pri_rows[:], ident[:])
+            nc.scalar.copy(pri_sb[:], pri_ps[:, 0 : S // P])
+
+        late = {}
 
         def order_w4():
+            w4_both = keep.tile([P, 3 * K], U8, name="plane0", align_bytes=64)
+            late["w4"] = w4_both
+            w4_codes = w4_both[:, 0 : 2 * K]
+            w4_scale = w4_both[:, 2 * K : 3 * K]
             nc.vector.tensor_copy(
-                w4_codes[:].bitcast(U16).rearrange("p (t m) -> p t m", t=PACK),
+                w4_codes.bitcast(U16).rearrange("p (t m) -> p t m", t=PACK),
                 w4_raw[:].bitcast(U16).rearrange("p (m t) -> p t m", t=PACK),
             )
             nc.vector.tensor_copy(
-                w4_scale[:].rearrange("p (t m) -> p t m", t=PACK),
+                w4_scale.rearrange("p (t m) -> p t m", t=PACK),
                 s4_raw[:].rearrange("p (m t) -> p t m", t=PACK),
             )
 
-        low = [keep.tile([P, 2, HALF], F32, name="low%d" % u) for u in range(2)]
-        high = [keep.tile([P, 2, C], F32, name="high%d" % c) for c in range(NCH)]
+        low = [keep.tile([P, 2, HALF], F32, name="low%d" % u, align_bytes=64) for u in range(2)]
+        high = keep.tile([P, S], F32, name="high")
         xb = [keep.tile([P, C, PACK], BF16, name="xb%d" % c, align_bytes=64) for c in range(NCH)]
         xg_codes = keep.tile([P, S], U32, name="xg_codes", align_bytes=64)
         xg_scale = keep.tile([P, S], U8, name="xg_scale", align_bytes=64)
         h_codes = keep.tile([P, S], U32, name="h_codes", align_bytes=64)
         h_scale = keep.tile([P, S], U8, name="h_scale", align_bytes=64)
-        gate = [keep.tile([P, PACK, C], F32, name="gate%d" % c) for c in range(NCH)]
+        gate = {}
         hb = [keep.tile([P, P, PACK], BF16, name="hb%d" % b, align_bytes=64) for b in range(S // P)]
         prob = [keep.tile([P, S], F32, name="prob%d" % b) for b in range(S // P)]
-        w1b = keep.tile([P, PACK, P, PACK], BF16, name="w1b", align_bytes=64)
-        w1_codes = keep.tile([P, K], U32, name="w1_codes", align_bytes=64)
         w1_scale = keep.tile([P, K], U8, name="w1_scale", align_bytes=64)
 
         def gather(t, first, count):
             weights = wgt_sb[:, first : first + count]
             if t < 2:
                 dst = low[first // HALF][:, t, first % HALF : first % HALF + count]
+            elif first >= LAST:
+                dst = late["high"][:, t - 2, first - LAST : first - LAST + count]
+            elif t == 2:
+                dst = high[:, first : first + count]
             else:
-                dst = high[first // C][:, t - 2, first % C : first % C + count]
+                dst = high[:, LAST + first % C : LAST + first % C + count]
             nc.vector.tensor_tensor(dst, planes[t][:].indirect(offsets[:, first // 16 : (first + count) // 16]), weights, MULT)
 
         def weave_low(c):
@@ -109,7 +140,11 @@ def tile_list_gated_entity_matching_kernel(tc, xT, wgt, offs, w1, w4_words, w4_s
 
         def weave_high(c, v):
             part = slice(v * P, (v + 1) * P)
-            nc.vector.tensor_copy(xb[c][:, part, 2:4], high[c][:, :, part].rearrange("p t n -> p n t"))
+            if c == NCH - 1:
+                pair = late["high"][:, :, part]
+            else:
+                pair = high[:].rearrange("p (b n) -> p b n", n=P)[:, 2 * c + v : 2 * (NCH - 1) + v + 1 : 2 * (NCH - 1 - c), :]
+            nc.vector.tensor_copy(xb[c][:, part, 2:4], pair.rearrange("p t n -> p n t"))
 
         def quant_x(c):
             cols = slice(c * C, (c + 1) * C)
@@ -117,14 +152,15 @@ def tile_list_gated_entity_matching_kernel(tc, xT, wgt, offs, w1, w4_words, w4_s
 
         def gates(c):
             cols = slice(c * C, (c + 1) * C)
+            gate[c] = keep.tile([P, PACK, C], F32, name="w1_raw1" if c == 0 else "gate%d" % c)
             for u in range(2):
                 g = ps_g.tile([P, 2, C], F32, name="g")
                 for e in range(2):
                     t = 2 * u + e
                     nc.tensor.matmul_mx(
                         g[:, e, :],
-                        lhsT=w4_codes[:, 2 * P * t : 2 * P * (t + 1)].bitcast(FP4X4),
-                        lhsT_scale=w4_scale[:, P * t : P * (t + 1)],
+                        lhsT=late["w4"][:, 2 * P * t : 2 * P * (t + 1)].bitcast(FP4X4),
+                        lhsT_scale=late["w4"][:, 2 * K + P * t : 2 * K + P * (t + 1)],
                         rhs=xg_codes[:, cols].bitcast(FP8X4),
                         rhs_scale=xg_scale[:, cols],
                         start=True,
@@ -135,13 +171,18 @@ def tile_list_gated_entity_matching_kernel(tc, xT, wgt, offs, w1, w4_words, w4_s
                     nc.scalar.activation(gate[c][:, t, :], g[:, e, :], SIGMOID, bias=bg_sb[:, t : t + 1])
 
         def cast_w1(u):
-            (nc.scalar.copy, nc.vector.tensor_copy)[u](
+            if u == 0:
+                late["w1b"] = keep.tile([P, PACK, P, PACK], BF16, name="low1", align_bytes=64)
+            w1b = late["w1b"]
+            nc.scalar.copy(
                 w1b[:, :, u * P // 2 : (u + 1) * P // 2, :].rearrange("p t m j -> p m j t"),
                 w1_raw[u][:].rearrange("p j (m t) -> p m j t", t=PACK),
             )
 
         def quant_w1():
-            nc.vector.quantize_mx(w1_codes[:].bitcast(FP8X4), w1_scale[:], w1b[:].rearrange("p t m j -> p (t m j)"))
+            late["w1"] = keep.tile([P, K], U32, name="xb1", align_bytes=64)
+            w1_codes = late["w1"]
+            nc.vector.quantize_mx(w1_codes[:].bitcast(FP8X4), w1_scale[:], late["w1b"][:].rearrange("p t m j -> p (t m j)"))
 
         def gated(c, v):
             cols = slice(c * C + v * P, c * C + (v + 1) * P)
@@ -149,7 +190,7 @@ def tile_list_gated_entity_matching_kernel(tc, xT, wgt, offs, w1, w4_words, w4_s
             for t in range(PACK):
                 nc.tensor.matmul_mx(
                     a[:, t, :],
-                    lhsT=w1_codes[:, P * t : P * (t + 1)].bitcast(FP8X4),
+                    lhsT=late["w1"][:, P * t : P * (t + 1)].bitcast(FP8X4),
                     lhsT_scale=w1_scale[:, P * t : P * (t + 1)],
                     rhs=xg_codes[:, cols].bitcast(FP8X4),
                     rhs_scale=xg_scale[:, cols],
@@ -181,22 +222,22 @@ def tile_list_gated_entity_matching_kernel(tc, xT, wgt, offs, w1, w4_words, w4_s
                 stop=True,
             )
             nc.scalar.activation(prob[b][:, cols], y[:], SIGMOID, bias=pri_sb[:, b : b + 1])
-            if b == S // P - 1:
+            if b in (0, S // P - 1):
                 nc.sync.dma_start(out[rows, cols], prob[b][:, cols])
             elif u == 1:
                 nc.sync.dma_start(out[rows, :], prob[b][:])
 
-        gather(0, 0, C)
+        for first, count in pieces[:-1] + [(3, 1), (4, 1)]:
+            gather(0, first * P, count * P)
         order_w4()
-        gather(0, C, C)
-        gather(0, HALF, HALF)
         for u in range(2):
             gather(1, u * HALF, HALF)
             weave_low(2 * u)
             weave_low(2 * u + 1)
-        for c in range(NCH):
-            gather(2, c * C, C)
+        gather(2, 0, LAST)
+        turn_pri()
         cast_w1(0)
+        cast_w1(1)
         for c in range(NCH):
             for v in range(2):
                 gather(3, c * C + v * P, P)
@@ -204,10 +245,10 @@ def tile_list_gated_entity_matching_kernel(tc, xT, wgt, offs, w1, w4_words, w4_s
                 weave_high(c, v)
             quant_x(c)
             gates(c)
-            if c == 1:
-                cast_w1(1)
-            if c == 2:
+            if c == NCH - 2:
                 quant_w1()
+                late["high"] = keep.tile([P, 2, C], F32, name="low1", align_bytes=64)
+                gather(2, LAST, C)
         for b in range(S // P):
             gated(b // 2, b % 2)
             quant_h(b)

@@ -222,10 +222,7 @@ def tile_list_gated_entity_matching_kernel(tc, xT, wgt, offs, w1, w4_words, w4_s
                 stop=True,
             )
             nc.scalar.activation(prob[b][:, cols], y[:], SIGMOID, bias=pri_sb[:, b : b + 1])
-            if b in (0, S // P - 1):
-                nc.sync.dma_start(out[rows, cols], prob[b][:, cols])
-            elif u == 1:
-                nc.sync.dma_start(out[rows, :], prob[b][:])
+            nc.sync.dma_start(out[rows, cols], prob[b][:, cols])
 
         for first, count in pieces[:-1] + [(3, 1), (4, 1)]:
             gather(0, first * P, count * P)

@@ -111,14 +111,14 @@ def tile_list_gated_entity_matching_kernel(tc, xT, wgt, offs, w1, w4_words, w4_s
             )
 
         low = [keep.tile([P, 2, HALF], F32, name="low%d" % u, align_bytes=64) for u in range(2)]
-        high = keep.tile([P, S], F32, name="high")
+        high = keep.tile([P, LAST + 2 * C], F32, name="high")
         xb = [keep.tile([P, C, PACK], BF16, name="xb%d" % c, align_bytes=64) for c in range(NCH)]
         xg_codes = keep.tile([P, S], U32, name="xg_codes", align_bytes=64)
         xg_scale = keep.tile([P, S], U8, name="xg_scale", align_bytes=64)
         h_codes = keep.tile([P, S], U32, name="h_codes", align_bytes=64)
         h_scale = keep.tile([P, S], U8, name="h_scale", align_bytes=64)
         gate = {}
-        hb = [keep.tile([P, P, PACK], BF16, name="hb%d" % b, align_bytes=64) for b in range(S // P)]
+        hb = {}
         prob = [keep.tile([P, S], F32, name="prob%d" % b) for b in range(S // P)]
         w1_scale = keep.tile([P, K], U8, name="w1_scale", align_bytes=64)
 
@@ -131,28 +131,31 @@ def tile_list_gated_entity_matching_kernel(tc, xT, wgt, offs, w1, w4_words, w4_s
             elif t == 2:
                 dst = high[:, first : first + count]
             else:
-                dst = high[:, LAST + first % C : LAST + first % C + count]
+                dst = high[:, LAST + first % HALF : LAST + first % HALF + count]
             nc.vector.tensor_tensor(dst, planes[t][:].indirect(offsets[:, first // 16 : (first + count) // 16]), weights, MULT)
 
         def weave_low(c):
             part = slice(c * C % HALF, c * C % HALF + C)
             nc.scalar.copy(xb[c][:, :, 0:2], low[c * C // HALF][:, :, part].rearrange("p t n -> p n t"))
 
-        def weave_high(c, v):
-            part = slice(v * P, (v + 1) * P)
+        def weave_high(c, first=0, count=C):
+            part = slice(first, first + count)
             if c == NCH - 1:
                 pair = late["high"][:, :, part]
             else:
-                pair = high[:].rearrange("p (b n) -> p b n", n=P)[:, 2 * c + v : 2 * (NCH - 1) + v + 1 : 2 * (NCH - 1 - c), :]
+                slot = NCH - 1 + c % 2
+                pair = high[:].rearrange("p (b n) -> p b n", n=C)[:, c : slot + 1 : slot - c, part]
             nc.vector.tensor_copy(xb[c][:, part, 2:4], pair.rearrange("p t n -> p n t"))
 
-        def quant_x(c):
-            cols = slice(c * C, (c + 1) * C)
-            nc.vector.quantize_mx(xg_codes[:, cols].bitcast(FP8X4), xg_scale[:, cols], xb[c][:].rearrange("p n t -> p (n t)"))
+        def quant_x(c, first=0, count=C):
+            cols = slice(c * C + first, c * C + first + count)
+            nc.vector.quantize_mx(xg_codes[:, cols].bitcast(FP8X4), xg_scale[:, cols], xb[c][:, first : first + count, :].rearrange("p n t -> p (n t)"))
 
         def gates(c):
             cols = slice(c * C, (c + 1) * C)
-            gate[c] = keep.tile([P, PACK, C], F32, name="w1_raw1" if c == 0 else "gate%d" % c)
+            if c % 2 == 0:
+                both = keep.tile([P, 2, PACK, C], F32, name="w1_raw1" if c == 0 else "gate_late")
+                gate[c], gate[c + 1] = both[:, 0, :, :], both[:, 1, :, :]
             for u in range(2):
                 g = ps_g.tile([P, 2, C], F32, name="g")
                 for e in range(2):
@@ -187,6 +190,7 @@ def tile_list_gated_entity_matching_kernel(tc, xT, wgt, offs, w1, w4_words, w4_s
         def gated(c, v):
             cols = slice(c * C + v * P, c * C + (v + 1) * P)
             a = ps_a.tile([P, PACK, P], F32, name="a")
+            hb[2 * c + v] = keep.tile([P, P, PACK], BF16, name="low1" if c + v == 0 else "hb%d" % (2 * c + v), align_bytes=64)
             for t in range(PACK):
                 nc.tensor.matmul_mx(
                     a[:, t, :],
@@ -235,17 +239,28 @@ def tile_list_gated_entity_matching_kernel(tc, xT, wgt, offs, w1, w4_words, w4_s
         turn_pri()
         cast_w1(0)
         cast_w1(1)
-        for c in range(NCH):
-            for v in range(2):
-                gather(3, c * C + v * P, P)
-            for v in range(2):
-                weave_high(c, v)
-            quant_x(c)
-            gates(c)
-            if c == NCH - 2:
-                quant_w1()
-                late["high"] = keep.tile([P, 2, C], F32, name="low1", align_bytes=64)
-                gather(2, LAST, C)
+        gather(3, 0, C)
+        gather(3, C, C)
+        weave_high(0)
+        weave_high(1)
+        quant_x(0)
+        gates(0)
+        gather(3, 2 * C, C)
+        quant_x(1)
+        gates(1)
+        weave_high(2)
+        quant_w1()
+        quant_x(2)
+        gates(2)
+        late["high"] = keep.tile([P, 2, C], F32, name="low1", align_bytes=64)
+        gather(2, LAST, C)
+        for v in range(2):
+            gather(3, LAST + v * P, P)
+        for v in range(2):
+            weave_high(NCH - 1, v * P, P)
+        for v in range(2):
+            quant_x(NCH - 1, v * P, P)
+        gates(NCH - 1)
         for b in range(S // P):
             gated(b // 2, b % 2)
             quant_h(b)

@@ -29,6 +29,7 @@ def tile_list_gated_entity_matching_kernel(tc, xT, wgt, offs, w1, w4_words, w4_s
     nc = tc.nc
     with ExitStack() as ctx:
         keep = ctx.enter_context(tc.tile_pool(name="keep", bufs=1))
+        held = ctx.enter_context(tc.tile_pool(name="held", bufs=1))
         ps_g = ctx.enter_context(tc.psum_pool(name="ps_g", bufs=3))
         ps_a = ctx.enter_context(tc.psum_pool(name="ps_a", bufs=2))
         ps_y = ctx.enter_context(tc.psum_pool(name="ps_y", bufs=3))
@@ -42,6 +43,9 @@ def tile_list_gated_entity_matching_kernel(tc, xT, wgt, offs, w1, w4_words, w4_s
         nc.vector.memset(wgt_rows[32:64, :], 0.0)
         nc.vector.memset(wgt_rows[64:P, :], 0.0)
 
+        warm = keep.tile([P, 1], F32, name="warm")
+        nc.scalar.activation(warm[64:P, :], wgt_rows[64:P, 0:1], SIGMOID)
+
         s4_raw = keep.tile([P, K], U8, name="s4_raw", align_bytes=64)
         nc.gpsimd.memset(s4_raw[:].bitcast(I32), 0)
         bg_sb = keep.tile([P, PACK], F32, name="bg_sb")
@@ -53,7 +57,7 @@ def tile_list_gated_entity_matching_kernel(tc, xT, wgt, offs, w1, w4_words, w4_s
         wgt_sb = keep.tile([P, S], F32, name="wgt_sb")
         planes = [keep.tile([P, T], F32, name="plane%d" % t, align_bytes=64) for t in range(PACK)]
         w1_hbm = w1.rearrange("(p j) r -> p j r", j=PACK)
-        w1_raw = [keep.tile([P, PACK, K // 2], F32, name="w1_raw%d" % u) for u in range(2)]
+        w1_raw = [keep.tile([P, PACK, K // 2], F32, name="w1_raw0"), held.tile([P, PACK, K // 2], F32, name="w1_raw1", offset=0, align_bytes=64)]
         nc.sync.dma_start(planes[0][:], planes_hbm[0])
         nc.sync.dma_start(offsets[:], offs)
         nc.sync.dma_start(w4_raw[:].bitcast(I32), w4_words[0].bitcast(I32))
@@ -114,7 +118,12 @@ def tile_list_gated_entity_matching_kernel(tc, xT, wgt, offs, w1, w4_words, w4_s
         high = keep.tile([P, LAST + 2 * C], F32, name="high")
         xb = [keep.tile([P, C, PACK], BF16, name="xb%d" % c, align_bytes=64) for c in range(NCH)]
         xg_codes = keep.tile([P, S], U32, name="xg_codes", align_bytes=64)
-        xg_scale = keep.tile([P, S], U8, name="xg_scale", align_bytes=64)
+        xg_scales = {0: keep.tile([P, HALF], U8, name="xg_scale0", align_bytes=64)}
+
+        def xg_scale(cols):
+            u = cols.start // HALF
+            return xg_scales[u][:, cols.start - u * HALF : cols.stop - u * HALF]
+
         h_codes = keep.tile([P, S], U32, name="h_codes", align_bytes=64)
         h_scale = keep.tile([P, S], U8, name="h_scale", align_bytes=64)
         gate = {}
@@ -149,12 +158,15 @@ def tile_list_gated_entity_matching_kernel(tc, xT, wgt, offs, w1, w4_words, w4_s
 
         def quant_x(c, first=0, count=C):
             cols = slice(c * C + first, c * C + first + count)
-            nc.vector.quantize_mx(xg_codes[:, cols].bitcast(FP8X4), xg_scale[:, cols], xb[c][:, first : first + count, :].rearrange("p n t -> p (n t)"))
+            nc.vector.quantize_mx(xg_codes[:, cols].bitcast(FP8X4), xg_scale(cols), xb[c][:, first : first + count, :].rearrange("p n t -> p (n t)"))
 
         def gates(c):
             cols = slice(c * C, (c + 1) * C)
             if c % 2 == 0:
-                both = keep.tile([P, 2, PACK, C], F32, name="w1_raw1" if c == 0 else "gate_late")
+                if c == 0:
+                    both = held.tile([P, 2, PACK, C], F32, name="gate_early", offset=2560, align_bytes=64)
+                else:
+                    both = keep.tile([P, 2, PACK, C], F32, name="gate_late")
                 gate[c], gate[c + 1] = both[:, 0, :, :], both[:, 1, :, :]
             for u in range(2):
                 g = ps_g.tile([P, 2, C], F32, name="g")
@@ -165,7 +177,7 @@ def tile_list_gated_entity_matching_kernel(tc, xT, wgt, offs, w1, w4_words, w4_s
                         lhsT=late["w4"][:, 2 * P * t : 2 * P * (t + 1)].bitcast(FP4X4),
                         lhsT_scale=late["w4"][:, 2 * K + P * t : 2 * K + P * (t + 1)],
                         rhs=xg_codes[:, cols].bitcast(FP8X4),
-                        rhs_scale=xg_scale[:, cols],
+                        rhs_scale=xg_scale(cols),
                         start=True,
                         stop=True,
                     )
@@ -190,14 +202,17 @@ def tile_list_gated_entity_matching_kernel(tc, xT, wgt, offs, w1, w4_words, w4_s
         def gated(c, v):
             cols = slice(c * C + v * P, c * C + (v + 1) * P)
             a = ps_a.tile([P, PACK, P], F32, name="a")
-            hb[2 * c + v] = keep.tile([P, P, PACK], BF16, name="low1" if c + v == 0 else "hb%d" % (2 * c + v), align_bytes=64)
+            if c + v == 0:
+                hb[0] = held.tile([P, P, PACK], BF16, name="hb0", offset=0, align_bytes=64)
+            else:
+                hb[2 * c + v] = keep.tile([P, P, PACK], BF16, name="hb%d" % (2 * c + v), align_bytes=64)
             for t in range(PACK):
                 nc.tensor.matmul_mx(
                     a[:, t, :],
                     lhsT=late["w1"][:, P * t : P * (t + 1)].bitcast(FP8X4),
                     lhsT_scale=w1_scale[:, P * t : P * (t + 1)],
                     rhs=xg_codes[:, cols].bitcast(FP8X4),
-                    rhs_scale=xg_scale[:, cols],
+                    rhs_scale=xg_scale(cols),
                     start=True,
                     stop=True,
                 )
@@ -221,7 +236,7 @@ def tile_list_gated_entity_matching_kernel(tc, xT, wgt, offs, w1, w4_words, w4_s
                 lhsT=h_codes[:, rows].bitcast(FP8X4),
                 lhsT_scale=h_scale[:, rows],
                 rhs=xg_codes[:, cols].bitcast(FP8X4),
-                rhs_scale=xg_scale[:, cols],
+                rhs_scale=xg_scale(cols),
                 start=True,
                 stop=True,
             )
@@ -250,9 +265,10 @@ def tile_list_gated_entity_matching_kernel(tc, xT, wgt, offs, w1, w4_words, w4_s
         gates(1)
         weave_high(2)
         quant_w1()
+        xg_scales[1] = held.tile([P, HALF], U8, name="xg_scale1", offset=2048, align_bytes=64)
         quant_x(2)
         gates(2)
-        late["high"] = keep.tile([P, 2, C], F32, name="low1", align_bytes=64)
+        late["high"] = held.tile([P, 2, C], F32, name="high_late", offset=0, align_bytes=64)
         gather(2, LAST, C)
         for v in range(2):
             gather(3, LAST + v * P, P)

@@ -160,7 +160,7 @@ def tile_list_gated_entity_matching_kernel(tc, xT, wgt, offs, w1, w4_words, w4_s
             cols = slice(c * C + first, c * C + first + count)
             nc.vector.quantize_mx(xg_codes[:, cols].bitcast(FP8X4), xg_scale(cols), xb[c][:, first : first + count, :].rearrange("p n t -> p (n t)"))
 
-        def gates(c):
+        def gates(c, pairs=(0, 1)):
             cols = slice(c * C, (c + 1) * C)
             if c % 2 == 0:
                 if c == 0:
@@ -168,7 +168,7 @@ def tile_list_gated_entity_matching_kernel(tc, xT, wgt, offs, w1, w4_words, w4_s
                 else:
                     both = keep.tile([P, 2, PACK, C], F32, name="gate_late")
                 gate[c], gate[c + 1] = both[:, 0, :, :], both[:, 1, :, :]
-            for u in range(2):
+            for u in pairs:
                 g = ps_g.tile([P, 2, C], F32, name="g")
                 for e in range(2):
                     t = 2 * u + e
@@ -202,10 +202,7 @@ def tile_list_gated_entity_matching_kernel(tc, xT, wgt, offs, w1, w4_words, w4_s
         def gated(c, v):
             cols = slice(c * C + v * P, c * C + (v + 1) * P)
             a = ps_a.tile([P, PACK, P], F32, name="a")
-            if c + v == 0:
-                hb[0] = held.tile([P, P, PACK], BF16, name="hb0", offset=0, align_bytes=64)
-            else:
-                hb[2 * c + v] = keep.tile([P, P, PACK], BF16, name="hb%d" % (2 * c + v), align_bytes=64)
+            hb[2 * c + v] = keep.tile([P, P, PACK], BF16, name="hb%d" % (1 if 2 * c + v == 2 else 2 * c + v), align_bytes=64)
             for t in range(PACK):
                 nc.tensor.matmul_mx(
                     a[:, t, :],
@@ -272,12 +269,18 @@ def tile_list_gated_entity_matching_kernel(tc, xT, wgt, offs, w1, w4_words, w4_s
         gather(2, LAST, C)
         for v in range(2):
             gather(3, LAST + v * P, P)
+        gated(0, 0)
         for v in range(2):
             weave_high(NCH - 1, v * P, P)
+        quant_h(0)
+        match(0, 0)
         for v in range(2):
             quant_x(NCH - 1, v * P, P)
-        gates(NCH - 1)
-        for b in range(S // P):
+        gates(NCH - 1, (0,))
+        match(0, 1)
+        for b in range(1, S // P):
+            if b == NCH:
+                gates(NCH - 1, (1,))
             gated(b // 2, b % 2)
             quant_h(b)
             for u in range(2):

@@ -77,7 +77,7 @@ def tile_list_gated_entity_matching_kernel(tc, xT, wgt, offs, w1, w4_words, w4_s
         wgt_t = ps_y.tile([P, 2, P], F32, name="y")
         for e in range(2):
             nc.tensor.transpose(wgt_t[:, e, :], wgt_rows[:, e * P : (e + 1) * P], ident[:])
-        spread = keep.tile([P, S // P, 8, 16], F32, name="spread")
+        spread = keep.tile([P, S // P, 8, 16], F32, name="spread", align_bytes=64)
         for first, count in [(0, 1), (1, 1), (2, 2), (4, 2), (6, 2)]:
             s, d, e = first // 4, first // 2 % 2, first % 2
             nc.vector.tensor_copy(
@@ -101,11 +101,11 @@ def tile_list_gated_entity_matching_kernel(tc, xT, wgt, offs, w1, w4_words, w4_s
         late = {}
 
         def order_w4():
-            w4_both = keep.tile([P, 3 * K], U8, name="plane0", align_bytes=64)
-            late["w4"] = w4_both
-            w4_codes = w4_both[:, 0 : 2 * K]
-            w4_scale = w4_both[:, 2 * K : 3 * K]
-            nc.vector.tensor_copy(
+            late["w4"] = keep.tile([P, 2 * K], U8, name="plane0", align_bytes=64)
+            late["s4"] = keep.tile([P, K], U8, name="spread", align_bytes=64)
+            w4_codes = late["w4"][:]
+            w4_scale = late["s4"][:]
+            nc.scalar.copy(
                 w4_codes.bitcast(U16).rearrange("p (t m) -> p t m", t=PACK),
                 w4_raw[:].bitcast(U16).rearrange("p (m t) -> p t m", t=PACK),
             )
@@ -175,7 +175,7 @@ def tile_list_gated_entity_matching_kernel(tc, xT, wgt, offs, w1, w4_words, w4_s
                     nc.tensor.matmul_mx(
                         g[:, e, :],
                         lhsT=late["w4"][:, 2 * P * t : 2 * P * (t + 1)].bitcast(FP4X4),
-                        lhsT_scale=late["w4"][:, 2 * K + P * t : 2 * K + P * (t + 1)],
+                        lhsT_scale=late["s4"][:, P * t : P * (t + 1)],
                         rhs=xg_codes[:, cols].bitcast(FP8X4),
                         rhs_scale=xg_scale(cols),
                         start=True,

@@ -49,8 +49,7 @@ def tile_list_gated_entity_matching_kernel(tc, xT, wgt, offs, w1, w4_words, w4_s
         s4_raw = keep.tile([P, K], U8, name="s4_raw", align_bytes=64)
         nc.gpsimd.memset(s4_raw[:].bitcast(I32), 0)
         bg_sb = keep.tile([P, PACK], F32, name="bg_sb")
-        pri_rows = keep.tile([P, P], F32, name="pri_rows")
-        nc.gpsimd.memset(pri_rows[:], 0.0)
+        pri_sb = keep.tile([P, S // P], F32, name="pri_sb")
 
         w4_raw = keep.tile([P, 2 * K], U8, name="w4_raw", align_bytes=64)
         planes_hbm = xT.rearrange("(p t) n -> t p n", t=PACK)
@@ -64,39 +63,31 @@ def tile_list_gated_entity_matching_kernel(tc, xT, wgt, offs, w1, w4_words, w4_s
         for q in range(4):
             nc.sync.dma_start(s4_raw[32 * q : 32 * q + 4, :].bitcast(I32), w4_scales[0, 4 * q : 4 * q + 4, :].bitcast(I32))
         nc.sync.dma_start(planes[1][:], planes_hbm[1])
-        nc.sync.dma_start(pri_rows[0 : S // P, :], pri.rearrange("(c p) -> c p", p=P))
-        nc.sync.dma_start(bg_sb[:], bg.rearrange("(p t) -> p t", t=PACK))
         nc.sync.dma_start(planes[2][:], planes_hbm[2])
         nc.sync.dma_start(planes[3][:], planes_hbm[3])
         nc.sync.dma_start(w1_raw[0][:], w1_hbm[:, :, 0 : K // 2])
         nc.sync.dma_start(w1_raw[1][:], w1_hbm[:, :, K // 2 : K])
+        nc.sync.dma_start(bg_sb[:], bg.rearrange("(p t) -> p t", t=PACK))
+        with nc.allow_non_contiguous_dma(reason="one value of pri for each partition and row block"):
+            nc.sync.dma_start(pri_sb[:], pri.rearrange("(c p) -> p c", p=P))
 
         ident = keep.tile([P, P], F32, name="ident")
         make_identity(nc, ident[:])
 
-        wgt_t = ps_y.tile([P, 2, P], F32, name="y")
+        wgt_t = [ps_y.tile([P, P], F32, name="y") for e in range(2)]
         for e in range(2):
-            nc.tensor.transpose(wgt_t[:, e, :], wgt_rows[:, e * P : (e + 1) * P], ident[:])
+            nc.tensor.transpose(wgt_t[e][:], wgt_rows[:, e * P : (e + 1) * P], ident[:])
         spread = keep.tile([P, S // P, 8, 16], F32, name="spread", align_bytes=64)
-        for first, count in [(0, 1), (1, 1), (2, 2), (4, 2), (6, 2)]:
+        for first, count in [(0, 1), (1, 1), (2, 1), (5, 2), (4, 2), (3, 1)]:
             s, d, e = first // 4, first // 2 % 2, first % 2
-            nc.vector.tensor_copy(
-                spread[:, first : first + count, :, :],
-                wgt_t[:, e : e + count, 16 * d + s : 16 * (d + 1) : 2].unsqueeze(3).to_broadcast([P, count, 8, 16]),
-            )
+            columns = wgt_t[e][:, 0:32].rearrange("p (d g s) -> p d g s", d=2, s=2)[:, d : d + count, :, s : s + 1]
+            nc.vector.tensor_copy(spread[:, first : first + 2 * count - 1 : 2, :, :], columns.to_broadcast([P, count, 8, 16]))
         pieces = [(0, 1), (1, 2), (5, 3), (3, 2)]
         for first, count in pieces:
             back = ps_g.tile([P, count, P], F32, name="g")
             for v in range(count):
                 nc.tensor.transpose(back[:, v, :], spread[:, first + v, :, :].rearrange("p g r -> p (g r)"), ident[:])
             nc.scalar.copy(wgt_sb[:, first * P : (first + count) * P], back[:].rearrange("p v n -> p (v n)"))
-
-        pri_sb = keep.tile([P, S // P], F32, name="pri_sb")
-
-        def turn_pri():
-            pri_ps = ps_g.tile([P, HALF], F32, name="g")
-            nc.tensor.transpose(pri_ps[:, 0:P], pri_rows[:], ident[:])
-            nc.scalar.copy(pri_sb[:], pri_ps[:, 0 : S // P])
 
         late = {}
 
@@ -114,7 +105,7 @@ def tile_list_gated_entity_matching_kernel(tc, xT, wgt, offs, w1, w4_words, w4_s
                 s4_raw[:].rearrange("p (m t) -> p t m", t=PACK),
             )
 
-        low = [keep.tile([P, 2, HALF], F32, name="low%d" % u, align_bytes=64) for u in range(2)]
+        low = keep.tile([P, 2 * S], F32, name="low", align_bytes=64)
         high = keep.tile([P, LAST + 2 * C], F32, name="high")
         xb = [keep.tile([P, C, PACK], BF16, name="xb%d" % c, align_bytes=64) for c in range(NCH)]
         xg_codes = keep.tile([P, S], U32, name="xg_codes", align_bytes=64)
@@ -134,7 +125,7 @@ def tile_list_gated_entity_matching_kernel(tc, xT, wgt, offs, w1, w4_words, w4_s
         def gather(t, first, count):
             weights = wgt_sb[:, first : first + count]
             if t < 2:
-                dst = low[first // HALF][:, t, first % HALF : first % HALF + count]
+                dst = low[:, t * S + first : t * S + first + count]
             elif first >= LAST:
                 dst = late["high"][:, t - 2, first - LAST : first - LAST + count]
             elif t == 2:
@@ -144,8 +135,8 @@ def tile_list_gated_entity_matching_kernel(tc, xT, wgt, offs, w1, w4_words, w4_s
             nc.vector.tensor_tensor(dst, planes[t][:].indirect(offsets[:, first // 16 : (first + count) // 16]), weights, MULT)
 
         def weave_low(c):
-            part = slice(c * C % HALF, c * C % HALF + C)
-            nc.scalar.copy(xb[c][:, :, 0:2], low[c * C // HALF][:, :, part].rearrange("p t n -> p n t"))
+            pair = low[:].rearrange("p (b n) -> p b n", n=C)[:, c : c + NCH + 1 : NCH, :]
+            nc.scalar.copy(xb[c][:, :, 0:2], pair.rearrange("p t n -> p n t"))
 
         def weave_high(c, first=0, count=C):
             part = slice(first, first + count)
@@ -187,7 +178,7 @@ def tile_list_gated_entity_matching_kernel(tc, xT, wgt, offs, w1, w4_words, w4_s
 
         def cast_w1(u):
             if u == 0:
-                late["w1b"] = keep.tile([P, PACK, P, PACK], BF16, name="low1", align_bytes=64)
+                late["w1b"] = keep.tile([P, PACK, P, PACK], BF16, name="low", align_bytes=64)
             w1b = late["w1b"]
             nc.scalar.copy(
                 w1b[:, :, u * P // 2 : (u + 1) * P // 2, :].rearrange("p t m j -> p m j t"),
@@ -240,7 +231,7 @@ def tile_list_gated_entity_matching_kernel(tc, xT, wgt, offs, w1, w4_words, w4_s
             nc.scalar.activation(prob[b][:, cols], y[:], SIGMOID, bias=pri_sb[:, b : b + 1])
             nc.sync.dma_start(out[rows, cols], prob[b][:, cols])
 
-        for first, count in pieces[:-1] + [(3, 1), (4, 1)]:
+        for first, count in pieces:
             gather(0, first * P, count * P)
         order_w4()
         for u in range(2):
@@ -248,7 +239,6 @@ def tile_list_gated_entity_matching_kernel(tc, xT, wgt, offs, w1, w4_words, w4_s
             weave_low(2 * u)
             weave_low(2 * u + 1)
         gather(2, 0, LAST)
-        turn_pri()
         cast_w1(0)
         cast_w1(1)
         gather(3, 0, C)

@@ -23,6 +23,8 @@ C = 256
 NCH = S // C
 HALF = 512
 LAST = S - C
+SECOND = (0, 1, 2, 0)
+THIRD = (3, 4, 3, 5)
 
 
 def tile_list_gated_entity_matching_kernel(tc, xT, wgt, offs, w1, w4_words, w4_scales, bg, pri, out):
@@ -30,6 +32,7 @@ def tile_list_gated_entity_matching_kernel(tc, xT, wgt, offs, w1, w4_words, w4_s
     with ExitStack() as ctx:
         keep = ctx.enter_context(tc.tile_pool(name="keep", bufs=1))
         held = ctx.enter_context(tc.tile_pool(name="held", bufs=1))
+        held0 = ctx.enter_context(tc.tile_pool(name="held0", bufs=1))
         ps_g = ctx.enter_context(tc.psum_pool(name="ps_g", bufs=3))
         ps_a = ctx.enter_context(tc.psum_pool(name="ps_a", bufs=2))
         ps_y = ctx.enter_context(tc.psum_pool(name="ps_y", bufs=3))
@@ -49,27 +52,29 @@ def tile_list_gated_entity_matching_kernel(tc, xT, wgt, offs, w1, w4_words, w4_s
         s4_raw = keep.tile([P, K], U8, name="s4_raw", align_bytes=64)
         nc.gpsimd.memset(s4_raw[:].bitcast(I32), 0)
         bg_sb = keep.tile([P, PACK], F32, name="bg_sb")
-        pri_sb = keep.tile([P, S // P], F32, name="pri_sb")
+        pri_rows = keep.tile([P, P], F32, name="pri_rows")
+        nc.gpsimd.memset(pri_rows[:], 0.0)
 
         w4_raw = keep.tile([P, 2 * K], U8, name="w4_raw", align_bytes=64)
         planes_hbm = xT.rearrange("(p t) n -> t p n", t=PACK)
         wgt_sb = keep.tile([P, S], F32, name="wgt_sb")
         planes = [keep.tile([P, T], F32, name="plane%d" % t, align_bytes=64) for t in range(PACK)]
         w1_hbm = w1.rearrange("(p j) r -> p j r", j=PACK)
-        w1_raw = [keep.tile([P, PACK, K // 2], F32, name="w1_raw0"), held.tile([P, PACK, K // 2], F32, name="w1_raw1", offset=0, align_bytes=64)]
+        high = keep.tile([P, 5 * C + PACK * K // 2], F32, name="high")
+        w1_first = held0.tile([P, PACK, K // 2], F32, name="w1_first", offset=0, align_bytes=64)
+        w1_raw = [w1_first[:], high[:, 5 * C :].rearrange("p (j r) -> p j r", j=PACK)]
         nc.sync.dma_start(planes[0][:], planes_hbm[0])
         nc.sync.dma_start(offsets[:], offs)
         nc.sync.dma_start(w4_raw[:].bitcast(I32), w4_words[0].bitcast(I32))
         for q in range(4):
             nc.sync.dma_start(s4_raw[32 * q : 32 * q + 4, :].bitcast(I32), w4_scales[0, 4 * q : 4 * q + 4, :].bitcast(I32))
         nc.sync.dma_start(planes[1][:], planes_hbm[1])
+        nc.sync.dma_start(pri_rows[0 : S // P, :], pri.rearrange("(c p) -> c p", p=P))
+        nc.sync.dma_start(bg_sb[:], bg.rearrange("(p t) -> p t", t=PACK))
         nc.sync.dma_start(planes[2][:], planes_hbm[2])
         nc.sync.dma_start(planes[3][:], planes_hbm[3])
-        nc.sync.dma_start(w1_raw[0][:], w1_hbm[:, :, 0 : K // 2])
-        nc.sync.dma_start(w1_raw[1][:], w1_hbm[:, :, K // 2 : K])
-        nc.sync.dma_start(bg_sb[:], bg.rearrange("(p t) -> p t", t=PACK))
-        with nc.allow_non_contiguous_dma(reason="one value of pri for each partition and row block"):
-            nc.sync.dma_start(pri_sb[:], pri.rearrange("(c p) -> p c", p=P))
+        nc.sync.dma_start(w1_raw[0], w1_hbm[:, :, 0 : K // 2])
+        nc.sync.dma_start(w1_raw[1], w1_hbm[:, :, K // 2 : K])
 
         ident = keep.tile([P, P], F32, name="ident")
         make_identity(nc, ident[:])
@@ -89,7 +94,15 @@ def tile_list_gated_entity_matching_kernel(tc, xT, wgt, offs, w1, w4_words, w4_s
                 nc.tensor.transpose(back[:, v, :], spread[:, first + v, :, :].rearrange("p g r -> p (g r)"), ident[:])
             nc.scalar.copy(wgt_sb[:, first * P : (first + count) * P], back[:].rearrange("p v n -> p (v n)"))
 
+        pri_sb = keep.tile([P, S // P], F32, name="pri_sb")
+
+        def turn_pri():
+            pri_ps = ps_g.tile([P, HALF], F32, name="g")
+            nc.tensor.transpose(pri_ps[:, 0:P], pri_rows[:], ident[:])
+            nc.scalar.copy(pri_sb[:], pri_ps[:, 0 : S // P])
+
         late = {}
+
 
         def order_w4():
             late["w4"] = keep.tile([P, 2 * K], U8, name="plane0", align_bytes=64)
@@ -105,8 +118,7 @@ def tile_list_gated_entity_matching_kernel(tc, xT, wgt, offs, w1, w4_words, w4_s
                 s4_raw[:].rearrange("p (m t) -> p t m", t=PACK),
             )
 
-        low = keep.tile([P, 2 * S], F32, name="low", align_bytes=64)
-        high = keep.tile([P, LAST + 2 * C], F32, name="high")
+        low = held.tile([P, 2 * S], F32, name="low", offset=0, align_bytes=64)
         xb = [keep.tile([P, C, PACK], BF16, name="xb%d" % c, align_bytes=64) for c in range(NCH)]
         xg_codes = keep.tile([P, S], U32, name="xg_codes", align_bytes=64)
         xg_scales = {0: keep.tile([P, HALF], U8, name="xg_scale0", align_bytes=64)}
@@ -126,12 +138,9 @@ def tile_list_gated_entity_matching_kernel(tc, xT, wgt, offs, w1, w4_words, w4_s
             weights = wgt_sb[:, first : first + count]
             if t < 2:
                 dst = low[:, t * S + first : t * S + first + count]
-            elif first >= LAST:
-                dst = late["high"][:, t - 2, first - LAST : first - LAST + count]
-            elif t == 2:
-                dst = high[:, first : first + count]
             else:
-                dst = high[:, LAST + first % HALF : LAST + first % HALF + count]
+                place = (SECOND if t == 2 else THIRD)[first // C] * C + first % C
+                dst = high[:, place : place + count]
             nc.vector.tensor_tensor(dst, planes[t][:].indirect(offsets[:, first // 16 : (first + count) // 16]), weights, MULT)
 
         def weave_low(c):
@@ -140,11 +149,7 @@ def tile_list_gated_entity_matching_kernel(tc, xT, wgt, offs, w1, w4_words, w4_s
 
         def weave_high(c, first=0, count=C):
             part = slice(first, first + count)
-            if c == NCH - 1:
-                pair = late["high"][:, :, part]
-            else:
-                slot = NCH - 1 + c % 2
-                pair = high[:].rearrange("p (b n) -> p b n", n=C)[:, c : slot + 1 : slot - c, part]
+            pair = high[:].rearrange("p (b n) -> p b n", n=C)[:, SECOND[c] : THIRD[c] + 1 : THIRD[c] - SECOND[c], part]
             nc.vector.tensor_copy(xb[c][:, part, 2:4], pair.rearrange("p t n -> p n t"))
 
         def quant_x(c, first=0, count=C):
@@ -155,7 +160,7 @@ def tile_list_gated_entity_matching_kernel(tc, xT, wgt, offs, w1, w4_words, w4_s
             cols = slice(c * C, (c + 1) * C)
             if c % 2 == 0:
                 if c == 0:
-                    both = held.tile([P, 2, PACK, C], F32, name="gate_early", offset=2560, align_bytes=64)
+                    both = held0.tile([P, 2, PACK, C], F32, name="gate_early", offset=0, align_bytes=64)
                 else:
                     both = keep.tile([P, 2, PACK, C], F32, name="gate_late")
                 gate[c], gate[c + 1] = both[:, 0, :, :], both[:, 1, :, :]
@@ -178,11 +183,11 @@ def tile_list_gated_entity_matching_kernel(tc, xT, wgt, offs, w1, w4_words, w4_s
 
         def cast_w1(u):
             if u == 0:
-                late["w1b"] = keep.tile([P, PACK, P, PACK], BF16, name="low", align_bytes=64)
+                late["w1b"] = held.tile([P, PACK, P, PACK], BF16, name="w1b", offset=0, align_bytes=64)
             w1b = late["w1b"]
             nc.scalar.copy(
                 w1b[:, :, u * P // 2 : (u + 1) * P // 2, :].rearrange("p t m j -> p m j t"),
-                w1_raw[u][:].rearrange("p j (m t) -> p m j t", t=PACK),
+                w1_raw[u].rearrange("p j (m t) -> p m j t", t=PACK),
             )
 
         def quant_w1():
@@ -239,6 +244,7 @@ def tile_list_gated_entity_matching_kernel(tc, xT, wgt, offs, w1, w4_words, w4_s
             weave_low(2 * u)
             weave_low(2 * u + 1)
         gather(2, 0, LAST)
+        turn_pri()
         cast_w1(0)
         cast_w1(1)
         gather(3, 0, C)
@@ -251,14 +257,13 @@ def tile_list_gated_entity_matching_kernel(tc, xT, wgt, offs, w1, w4_words, w4_s
         quant_x(1)
         gates(1)
         weave_high(2)
+        gather(2, LAST, C)
         quant_w1()
-        xg_scales[1] = held.tile([P, HALF], U8, name="xg_scale1", offset=2048, align_bytes=64)
+        xg_scales[1] = held.tile([P, HALF], U8, name="xg_scale1", offset=0, align_bytes=64)
+        gather(3, LAST, P)
         quant_x(2)
         gates(2)
-        late["high"] = held.tile([P, 2, C], F32, name="high_late", offset=0, align_bytes=64)
-        gather(2, LAST, C)
-        for v in range(2):
-            gather(3, LAST + v * P, P)
+        gather(3, LAST + P, P)
         gated(0, 0)
         for v in range(2):
             weave_high(NCH - 1, v * P, P)

from contextlib import ExitStack

import concourse.mybir as mybir
from concourse.masks import make_identity

K, T, S = 512, 2048, 1024
FLOPS = 2 * K * K * S * 2 + 2 * K * S * S

F32 = mybir.dt.float32
BF16 = mybir.dt.bfloat16
I32 = mybir.dt.int32
U32 = mybir.dt.uint32
U16 = mybir.dt.uint16
U8 = mybir.dt.uint8
FP8X4 = mybir.dt.float8_e4m3fn_x4
FP4X4 = mybir.dt.float4_e2m1fn_x4
MULT = mybir.AluOpType.mult
SIGMOID = mybir.ActivationFunctionType.Sigmoid

P = 128
PACK = 4
C = 256
NCH = S // C
HALF = 512
LAST = S - C
SECOND = (0, 1, 2, 0)
THIRD = (3, 4, 3, 5)


def tile_list_gated_entity_matching_kernel(tc, xT, wgt, offs, w1, w4_words, w4_scales, bg, pri, out):
    nc = tc.nc
    with ExitStack() as ctx:
        keep = ctx.enter_context(tc.tile_pool(name="keep", bufs=1))
        held = ctx.enter_context(tc.tile_pool(name="held", bufs=1))
        held0 = ctx.enter_context(tc.tile_pool(name="held0", bufs=1))
        ps_g = ctx.enter_context(tc.psum_pool(name="ps_g", bufs=3))
        ps_a = ctx.enter_context(tc.psum_pool(name="ps_a", bufs=2))
        ps_y = ctx.enter_context(tc.psum_pool(name="ps_y", bufs=3))

        offsets = keep.tile([P, S // 16], U16, name="offsets")

        wgt_rows = keep.tile([P, C], F32, name="wgt_rows")
        half_rows = wgt.rearrange("p (s n) -> (p s) n", s=2)[0 : 2 * P : 17, :]
        for d in range(2):
            nc.sync.dma_start(wgt_rows[16 * d : 16 * (d + 1), :], half_rows[:, d * C : (d + 1) * C])
        nc.vector.memset(wgt_rows[32:64, :], 0.0)
        nc.vector.memset(wgt_rows[64:P, :], 0.0)

        warm = keep.tile([P, 1], F32, name="warm")
        nc.scalar.activation(warm[64:P, :], wgt_rows[64:P, 0:1], SIGMOID)

        s4_raw = keep.tile([P, K], U8, name="s4_raw", align_bytes=64)
        nc.gpsimd.memset(s4_raw[:].bitcast(I32), 0)
        bg_sb = keep.tile([P, PACK], F32, name="bg_sb")
        pri_rows = keep.tile([P, P], F32, name="pri_rows")
        nc.gpsimd.memset(pri_rows[:], 0.0)

        w4_raw = keep.tile([P, 2 * K], U8, name="w4_raw", align_bytes=64)
        planes_hbm = xT.rearrange("(p t) n -> t p n", t=PACK)
        wgt_sb = keep.tile([P, S], F32, name="wgt_sb")
        planes = [keep.tile([P, T], F32, name="plane%d" % t, align_bytes=64) for t in range(PACK)]
        w1_hbm = w1.rearrange("(p j) r -> p j r", j=PACK)
        high = keep.tile([P, 5 * C + PACK * K // 2], F32, name="high")
        w1_first = held0.tile([P, PACK, K // 2], F32, name="w1_first", offset=0, align_bytes=64)
        w1_raw = [w1_first[:], high[:, 5 * C :].rearrange("p (j r) -> p j r", j=PACK)]
        nc.sync.dma_start(planes[0][:], planes_hbm[0])
        nc.sync.dma_start(offsets[:], offs)
        nc.sync.dma_start(w4_raw[:].bitcast(I32), w4_words[0].bitcast(I32))
        for q in range(4):
            nc.sync.dma_start(s4_raw[32 * q : 32 * q + 4, :].bitcast(I32), w4_scales[0, 4 * q : 4 * q + 4, :].bitcast(I32))
        nc.sync.dma_start(planes[1][:], planes_hbm[1])
        nc.sync.dma_start(pri_rows[0 : S // P, :], pri.rearrange("(c p) -> c p", p=P))
        nc.sync.dma_start(bg_sb[:], bg.rearrange("(p t) -> p t", t=PACK))
        nc.sync.dma_start(planes[2][:], planes_hbm[2])
        nc.sync.dma_start(planes[3][:], planes_hbm[3])
        nc.sync.dma_start(w1_raw[0], w1_hbm[:, :, 0 : K // 2])
        nc.sync.dma_start(w1_raw[1], w1_hbm[:, :, K // 2 : K])

        ident = keep.tile([P, P], F32, name="ident")
        make_identity(nc, ident[:])

        wgt_t = [ps_y.tile([P, P], F32, name="y") for e in range(2)]
        for e in range(2):
            nc.tensor.transpose(wgt_t[e][:], wgt_rows[:, e * P : (e + 1) * P], ident[:])
        spread = keep.tile([P, S // P, 8, 16], F32, name="spread", align_bytes=64)
        for first, count in [(0, 1), (1, 1), (2, 1), (5, 2), (4, 2), (3, 1)]:
            s, d, e = first // 4, first // 2 % 2, first % 2
            columns = wgt_t[e][:, 0:32].rearrange("p (d g s) -> p d g s", d=2, s=2)[:, d : d + count, :, s : s + 1]
            nc.vector.tensor_copy(spread[:, first : first + 2 * count - 1 : 2, :, :], columns.to_broadcast([P, count, 8, 16]))
        pieces = [(0, 1), (1, 2), (5, 3), (3, 2)]
        for first, count in pieces:
            back = ps_g.tile([P, count, P], F32, name="g")
            for v in range(count):
                nc.tensor.transpose(back[:, v, :], spread[:, first + v, :, :].rearrange("p g r -> p (g r)"), ident[:])
            nc.scalar.copy(wgt_sb[:, first * P : (first + count) * P], back[:].rearrange("p v n -> p (v n)"))

        pri_sb = keep.tile([P, S // P], F32, name="pri_sb")

        def turn_pri():
            pri_ps = ps_g.tile([P, HALF], F32, name="g")
            nc.tensor.transpose(pri_ps[:, 0:P], pri_rows[:], ident[:])
            nc.scalar.copy(pri_sb[:], pri_ps[:, 0 : S // P])

        late = {}


        def order_w4():
            late["w4"] = keep.tile([P, 2 * K], U8, name="plane0", align_bytes=64)
            late["s4"] = keep.tile([P, K], U8, name="spread", align_bytes=64)
            w4_codes = late["w4"][:]
            w4_scale = late["s4"][:]
            nc.scalar.copy(
                w4_codes.bitcast(U16).rearrange("p (t m) -> p t m", t=PACK),
                w4_raw[:].bitcast(U16).rearrange("p (m t) -> p t m", t=PACK),
            )
            nc.vector.tensor_copy(
                w4_scale.rearrange("p (t m) -> p t m", t=PACK),
                s4_raw[:].rearrange("p (m t) -> p t m", t=PACK),
            )

        low = held.tile([P, 2 * S], F32, name="low", offset=0, align_bytes=64)
        xb = [keep.tile([P, C, PACK], BF16, name="xb%d" % c, align_bytes=64) for c in range(NCH)]
        xg_codes = keep.tile([P, S], U32, name="xg_codes", align_bytes=64)
        xg_scales = {0: keep.tile([P, HALF], U8, name="xg_scale0", align_bytes=64)}

        def xg_scale(cols):
            u = cols.start // HALF
            return xg_scales[u][:, cols.start - u * HALF : cols.stop - u * HALF]

        h_codes = keep.tile([P, S], U32, name="h_codes", align_bytes=64)
        h_scale = keep.tile([P, S], U8, name="h_scale", align_bytes=64)
        gate = {}
        hb = {}
        prob = [keep.tile([P, S], F32, name="prob%d" % b) for b in range(S // P)]
        w1_scale = keep.tile([P, K], U8, name="w1_scale", align_bytes=64)

        def gather(t, first, count):
            weights = wgt_sb[:, first : first + count]
            if t < 2:
                dst = low[:, t * S + first : t * S + first + count]
            else:
                place = (SECOND if t == 2 else THIRD)[first // C] * C + first % C
                dst = high[:, place : place + count]
            nc.vector.tensor_tensor(dst, planes[t][:].indirect(offsets[:, first // 16 : (first + count) // 16]), weights, MULT)

        def weave_low(c):
            pair = low[:].rearrange("p (b n) -> p b n", n=C)[:, c : c + NCH + 1 : NCH, :]
            nc.scalar.copy(xb[c][:, :, 0:2], pair.rearrange("p t n -> p n t"))

        def weave_high(c, first=0, count=C):
            part = slice(first, first + count)
            pair = high[:].rearrange("p (b n) -> p b n", n=C)[:, SECOND[c] : THIRD[c] + 1 : THIRD[c] - SECOND[c], part]
            nc.vector.tensor_copy(xb[c][:, part, 2:4], pair.rearrange("p t n -> p n t"))

        def quant_x(c, first=0, count=C):
            cols = slice(c * C + first, c * C + first + count)
            nc.vector.quantize_mx(xg_codes[:, cols].bitcast(FP8X4), xg_scale(cols), xb[c][:, first : first + count, :].rearrange("p n t -> p (n t)"))

        def gates(c, pairs=(0, 1)):
            cols = slice(c * C, (c + 1) * C)
            if c % 2 == 0:
                if c == 0:
                    both = held0.tile([P, 2, PACK, C], F32, name="gate_early", offset=0, align_bytes=64)
                else:
                    both = keep.tile([P, 2, PACK, C], F32, name="gate_late")
                gate[c], gate[c + 1] = both[:, 0, :, :], both[:, 1, :, :]
            for u in pairs:
                g = ps_g.tile([P, 2, C], F32, name="g")
                for e in range(2):
                    t = 2 * u + e
                    nc.tensor.matmul_mx(
                        g[:, e, :],
                        lhsT=late["w4"][:, 2 * P * t : 2 * P * (t + 1)].bitcast(FP4X4),
                        lhsT_scale=late["s4"][:, P * t : P * (t + 1)],
                        rhs=xg_codes[:, cols].bitcast(FP8X4),
                        rhs_scale=xg_scale(cols),
                        start=True,
                        stop=True,
                    )
                for e in range(2):
                    t = 2 * u + e
                    nc.scalar.activation(gate[c][:, t, :], g[:, e, :], SIGMOID, bias=bg_sb[:, t : t + 1])

        def cast_w1(u):
            if u == 0:
                late["w1b"] = held.tile([P, PACK, P, PACK], BF16, name="w1b", offset=0, align_bytes=64)
            w1b = late["w1b"]
            nc.scalar.copy(
                w1b[:, :, u * P // 2 : (u + 1) * P // 2, :].rearrange("p t m j -> p m j t"),
                w1_raw[u].rearrange("p j (m t) -> p m j t", t=PACK),
            )

        def quant_w1():
            late["w1"] = keep.tile([P, K], U32, name="xb1", align_bytes=64)
            w1_codes = late["w1"]
            nc.vector.quantize_mx(w1_codes[:].bitcast(FP8X4), w1_scale[:], late["w1b"][:].rearrange("p t m j -> p (t m j)"))

        def gated(c, v):
            cols = slice(c * C + v * P, c * C + (v + 1) * P)
            a = ps_a.tile([P, PACK, P], F32, name="a")
            hb[2 * c + v] = keep.tile([P, P, PACK], BF16, name="hb%d" % (1 if 2 * c + v == 2 else 2 * c + v), align_bytes=64)
            for t in range(PACK):
                nc.tensor.matmul_mx(
                    a[:, t, :],
                    lhsT=late["w1"][:, P * t : P * (t + 1)].bitcast(FP8X4),
                    lhsT_scale=w1_scale[:, P * t : P * (t + 1)],
                    rhs=xg_codes[:, cols].bitcast(FP8X4),
                    rhs_scale=xg_scale(cols),
                    start=True,
                    stop=True,
                )
            nc.vector.tensor_tensor(
                hb[2 * c + v][:].rearrange("p (b i) t -> p b t i", i=4),
                a[:].rearrange("p t (b i) -> p b t i", i=4),
                gate[c][:, :, v * P : (v + 1) * P].rearrange("p t (b i) -> p b t i", i=4),
                MULT,
            )

        def quant_h(b):
            cols = slice(b * P, (b + 1) * P)
            nc.vector.quantize_mx(h_codes[:, cols].bitcast(FP8X4), h_scale[:, cols], hb[b][:].rearrange("p n t -> p (n t)"))

        def match(b, u):
            rows = slice(b * P, (b + 1) * P)
            cols = slice(u * HALF, (u + 1) * HALF)
            y = ps_y.tile([P, HALF], F32, name="y")
            nc.tensor.matmul_mx(
                y[:],
                lhsT=h_codes[:, rows].bitcast(FP8X4),
                lhsT_scale=h_scale[:, rows],
                rhs=xg_codes[:, cols].bitcast(FP8X4),
                rhs_scale=xg_scale(cols),
                start=True,
                stop=True,
            )
            nc.scalar.activation(prob[b][:, cols], y[:], SIGMOID, bias=pri_sb[:, b : b + 1])
            nc.sync.dma_start(out[rows, cols], prob[b][:, cols])

        for first, count in pieces:
            gather(0, first * P, count * P)
        order_w4()
        for u in range(2):
            gather(1, u * HALF, HALF)
            weave_low(2 * u)
            weave_low(2 * u + 1)
        gather(2, 0, LAST)
        turn_pri()
        cast_w1(0)
        cast_w1(1)
        gather(3, 0, C)
        gather(3, C, C)
        weave_high(0)
        weave_high(1)
        quant_x(0)
        gates(0)
        gather(3, 2 * C, C)
        quant_x(1)
        gates(1)
        weave_high(2)
        gather(2, LAST, C)
        quant_w1()
        xg_scales[1] = held.tile([P, HALF], U8, name="xg_scale1", offset=0, align_bytes=64)
        gather(3, LAST, P)
        quant_x(2)
        gates(2)
        gather(3, LAST + P, P)
        gated(0, 0)
        for v in range(2):
            weave_high(NCH - 1, v * P, P)
        quant_h(0)
        match(0, 0)
        for v in range(2):
            quant_x(NCH - 1, v * P, P)
        gates(NCH - 1, (0,))
        match(0, 1)
        for b in range(1, S // P):
            if b == NCH:
                gates(NCH - 1, (1,))
            gated(b // 2, b % 2)
            quant_h(b)
            for u in range(2):
                match(b, u)
